import numpy as np
import ml_dtypes


def mxq(x, axis, fmt="e4m3"):
    dtype, down = {"e4m3": (ml_dtypes.float8_e4m3fn, 7), "e5m2": (ml_dtypes.float8_e5m2, 14)}[fmt]
    v = np.moveaxis(np.asarray(x, np.float32).astype(ml_dtypes.bfloat16).astype(np.float64), axis, -1)
    blocks = v.reshape(v.shape[:-1] + (-1, 32))
    amax = np.abs(blocks).max(-1, keepdims=True)
    byte = np.maximum(np.where(amax > 0, np.frexp(amax)[1] - 1 + 127, 0) - down, 1)
    scale = np.exp2(byte - 127.0)
    codes = (blocks / scale).astype(np.float32).astype(dtype).astype(np.float64)
    return np.moveaxis((codes * scale).reshape(v.shape), -1, axis)


WIDE = False


def mx_kscale(k):
    if not WIDE:
        return np.ones(k)
    levels = np.array([10, -10, 5, -5, 0])
    if k % 512:
        return np.exp2(np.random.permutation(np.resize(levels, k // 32))).repeat(32)
    a = np.empty((k // 512, 16))
    for p in range(k // 512):
        a[p, :8] = np.random.permutation(np.resize(levels, 8))
        for g in range(8):
            far = levels[np.abs(levels - a[p, g]) >= 10]
            a[p, g + 8] = far[np.random.randint(len(far))]
    return np.exp2(a.ravel()).repeat(32)


BF16 = ml_dtypes.bfloat16


def bf(x):
    return np.asarray(x, np.float32).astype(BF16)


def f64(x):
    return np.asarray(x).astype(np.float64)

def planes(Y):
    n, m = Y.shape
    b = f64(bf(Y)).reshape(n // 32, 32, m)
    amax = np.abs(b).max(1)
    byte = np.clip(np.where(amax > 0, np.frexp(amax)[1] - 1 + 127 - 7, 1), 1, 254)
    codes = (b * np.exp2(127.0 - byte)[:, None, :]).reshape(n, m).astype(np.float32).astype(ml_dtypes.float8_e4m3fn).view(np.uint8)
    words = codes.reshape(n // 512, 128, 4, m).transpose(0, 1, 3, 2)
    return np.ascontiguousarray(words), np.ascontiguousarray(byte.astype(np.uint8).reshape(n // 512, 16, m))


NODES, FAN, F, HID = 2048, 4, 512, 1024


def setup_inputs():
    rn = np.random.randn
    s = mx_kscale(F)
    t = mx_kscale(F)
    x = rn(NODES, F) * s
    neighbours = rn(NODES, FAN, F) * t
    w_self = 0.8 * rn(F, HID) / np.sqrt(F) / s[:, None]
    w_neigh = 0.8 * rn(F, HID) * np.sqrt(FAN / F) / t[:, None]
    skip = 0.7 * rn(NODES, HID)
    node_weight = np.exp(0.8 * rn(NODES))
    return {"x": bf(x), "neighbours": bf(neighbours), "w_self": bf(w_self),
            "w_neigh": bf(w_neigh), "skip": bf(skip), "node_weight": bf(node_weight)}

def reference(x, neighbours, w_self, w_neigh, skip, node_weight):
    nbar = f64(neighbours).sum(axis=1) / FAN
    a = mxq(f64(x), 1) @ mxq(f64(w_self), 0)
    b = mxq(nbar, 1) @ mxq(f64(w_neigh), 0)
    h = np.maximum(a + b, 0.0) + f64(skip)
    y = h * f64(node_weight)[:, None]
    Y = y.reshape(NODES, HID)
    words, scales = planes(Y)
    return y, words, scales

@@ -1,0 +1,282 @@
+from contextlib import ExitStack
+
+import concourse.mybir as mybir
+from concourse.masks import make_identity
+
+NODES, FAN, F, HID = 2048, 4, 512, 1024
+FLOPS = 2 * 2 * NODES * F * HID
+
+F32 = mybir.dt.float32
+BF16 = mybir.dt.bfloat16
+I32 = mybir.dt.int32
+U32 = mybir.dt.uint32
+U8 = mybir.dt.uint8
+FP8X4 = mybir.dt.float8_e4m3fn_x4
+ALU = mybir.AluOpType
+ACT = mybir.ActivationFunctionType
+
+P = 128
+PACK = 4
+GROUP = P * PACK
+GROUPS = NODES // GROUP
+HALF = 512
+HALVES = HID // HALF
+UNITS = GROUPS * HALVES
+CHUNK_NODES = P // FAN
+CHUNKS_PER_LOAD = 8
+CHUNKS_PER_BANK = 4
+
+
+def tile_graphsage_mean_skip_layer_g2_kernel(
+    tc, x, neighbours, w_self, w_neigh, skip, node_weight, out_0, out_1, out_2
+):
+    nc = tc.nc
+    with ExitStack() as ctx:
+        keep = ctx.enter_context(tc.tile_pool(name="keep", bufs=1))
+        stream = ctx.enter_context(tc.tile_pool(name="stream", bufs=2))
+        psum = ctx.enter_context(tc.psum_pool(name="psum", bufs=4))
+        ctx.enter_context(tc.manual_schedule())
+
+        nb_rows = neighbours.rearrange("v n f -> (v n) f")
+        tiles = {}
+
+        def load_weight(name, w):
+            raw = stream.tile([P, PACK, HID], BF16, name="raw_" + name, tag="raw", bufs=6)
+            nc.sync.dma_start(out=raw[:], in_=w.rearrange("(p j) n -> p j n", j=PACK))
+            tiles["w_raw", name] = raw
+
+        def load_group(g):
+            rows = slice(g * GROUP, (g + 1) * GROUP)
+            x_raw = stream.tile([P, PACK, F], BF16, name="x_raw%d" % g, tag="x_raw", bufs=2)
+            nc.sync.dma_start(out=x_raw[:], in_=x[rows, :].rearrange("(p t) f -> p t f", t=PACK))
+            tiles["x_raw", g] = x_raw
+            n_rows = CHUNKS_PER_LOAD * P
+            for a in range(2):
+                nb_raw = stream.tile(
+                    [P, CHUNKS_PER_LOAD, F], BF16, name="nb_raw%d_%d" % (g, a), tag="raw", bufs=6
+                )
+                r0 = (2 * g + a) * n_rows
+                nc.sync.dma_start(
+                    out=nb_raw[:], in_=nb_rows[r0 : r0 + n_rows, :].rearrange("(c q) f -> q c f", q=P)
+                )
+                tiles["nb_raw", g, a] = nb_raw
+            skip_raw = stream.tile([P, PACK, HID], BF16, name="skip%d" % g, tag="skip", bufs=3)
+            nc.sync.dma_start(out=skip_raw[:], in_=skip[rows, :].rearrange("(p t) m -> p t m", t=PACK))
+            tiles["skip", g] = skip_raw
+
+        def quantize(key, staged, tag, bufs):
+            codes = stream.tile([P, HALF], U32, name="codes_" + tag, tag="codes_" + tag, bufs=bufs, align_bytes=64)
+            scales = stream.tile([P, HALF], U8, name="scales_" + tag, tag="scales_" + tag, bufs=bufs, align_bytes=64)
+            nc.vector.quantize_mx(out=codes[:].bitcast(FP8X4), scales=scales[:], in_=staged[:])
+            tiles[key] = (codes, scales)
+
+        def staged_tile(tag, bufs):
+            return stream.tile([P, HALF * PACK], BF16, name=tag, tag=tag, bufs=bufs, align_bytes=64)
+
+        def interleave(key, src):
+            staged = staged_tile("staged", 4)
+            nc.vector.tensor_copy(
+                out=staged[:].rearrange("p (m j) -> p m j", j=PACK), in_=src.rearrange("p j m -> p m j")
+            )
+            tiles[key] = staged
+
+        def interleave_weight(name, h):
+            interleave(("w_staged", name, h), tiles["w_raw", name][:, :, h * HALF : (h + 1) * HALF])
+
+        def quantize_weight(name, h):
+            quantize(("w", name, h), tiles["w_staged", name, h], "w", 4)
+
+        def turn_x(g, a):
+            bank = psum.tile([P, 2, 2, P], F32, name="x_bank", tag="turn")
+            for s in range(2):
+                words = tiles["x_raw", g][:, 2 * a + s, :].bitcast(F32)
+                for u in range(2):
+                    nc.tensor.transpose(bank[:, s, u, :], words[:, u : F // 2 : 2], ident[:])
+            tiles["x_bank", g, a] = bank
+
+        def copy_x(g, a):
+            if a == 0:
+                tiles["x_staged", g] = staged_tile("x_staged", 2)
+            dst = tiles["x_staged", g][:].bitcast(F32).rearrange("k (t p u) -> k t p u", t=PACK, u=2)
+            nc.scalar.copy(
+                out=dst[:, 2 * a : 2 * a + 2, :, :], in_=tiles["x_bank", g, a][:].rearrange("k s u p -> k s p u")
+            )
+
+        def mean_nb(g, b):
+            bank = psum.tile([P, PACK, PACK, CHUNKS_PER_BANK, 8], F32, name="nb_bank", tag="turn")
+            nb_raw = tiles["nb_raw", g, b // 2]
+            for c in range(CHUNKS_PER_BANK):
+                chunk = (b % 2) * CHUNKS_PER_BANK + c
+                for j in range(PACK):
+                    nc.tensor.matmul(
+                        bank[:, j, :, c, :], lhsT=nb_raw[:, chunk, j:F:PACK], rhs=mean_of[:], start=True, stop=True
+                    )
+            tiles["nb_bank", g, b] = bank
+
+        def copy_nb(g, b):
+            if b == 0:
+                tiles["nb_staged", g] = staged_tile("nb_staged", 2)
+            dst = tiles["nb_staged", g][:].rearrange("k (t p j) -> k t p j", t=PACK, j=PACK)
+            nc.scalar.copy(
+                out=dst[:, :, 32 * b : 32 * b + 32, :],
+                in_=tiles["nb_bank", g, b][:].rearrange("k j t c i -> k t (c i) j"),
+            )
+
+        def quantize_x(g):
+            quantize(("act", "self", g), tiles["x_staged", g], "x", 2)
+
+        def quantize_nb(g):
+            quantize(("act", "neigh", g), tiles["nb_staged", g], "nb", 2)
+
+        def products(u, t):
+            g, h = divmod(u, HALVES)
+            acc = psum.tile([P, HALF], F32, name="acc", tag="acc")
+            cols = slice(t * P, (t + 1) * P)
+            for i, name in enumerate(("self", "neigh")):
+                a_codes, a_scales = tiles["act", name, g]
+                w_codes, w_scales = tiles["w", name, h]
+                nc.tensor.matmul_mx(
+                    out=acc[:],
+                    lhsT=a_codes[:, cols].bitcast(FP8X4),
+                    lhsT_scale=a_scales[:, cols],
+                    rhs=w_codes[:].bitcast(FP8X4),
+                    rhs_scale=w_scales[:],
+                    start=(i == 0),
+                    stop=(i == 1),
+                )
+            tiles["acc", u, t] = acc
+
+        def epilogue(u, t):
+            g, h = divmod(u, HALVES)
+            if t == 0:
+                tiles["y", u] = stream.tile([P, PACK, HALF], F32, name="y", tag="y", bufs=UNITS)
+            y = tiles["y", u]
+            nc.vector.scalar_tensor_tensor(
+                out=y[:, t, :],
+                in0=tiles["acc", u, t][:],
+                scalar=0.0,
+                in1=tiles["skip", g][:, t, h * HALF : (h + 1) * HALF],
+                op0=ALU.max,
+                op1=ALU.add,
+            )
+            nc.scalar.activation(
+                out=y[:, t, :], in_=y[:, t, :], func=ACT.Copy, scale=weight[:, g * PACK + t : g * PACK + t + 1]
+            )
+
+        def interleave_y(u):
+            interleave(("y_staged", u), tiles["y", u][:])
+
+        def quantize_y(u):
+            g, h = divmod(u, HALVES)
+            if h == 0:
+                tiles["y_codes", g] = stream.tile(
+                    [P, HID], U32, name="y_codes", tag="y_codes", bufs=GROUPS, align_bytes=64
+                )
+            cols = slice(h * HALF, (h + 1) * HALF)
+            nc.vector.quantize_mx(
+                out=tiles["y_codes", g][:, cols].bitcast(FP8X4),
+                scales=y_scales[PACK * g : P, cols],
+                in_=tiles["y_staged", u][:],
+            )
+
+        def store_y(u):
+            g, h = divmod(u, HALVES)
+            dst = out_0[g * GROUP : (g + 1) * GROUP, h * HALF : (h + 1) * HALF]
+            nc.sync.dma_start(out=dst.rearrange("(p t) m -> p t m", t=PACK), in_=tiles["y", u][:])
+
+        def store_codes(g, cols):
+            dst = out_1[g].rearrange("p m t -> p (m t)").bitcast(I32)
+            nc.sync.dma_start(out=dst[:, cols], in_=tiles["y_codes", g][:, cols].bitcast(I32))
+
+        weight_raw = keep.tile([P, GROUPS, PACK], BF16)
+        nc.scalar.dma_start(out=weight_raw[:], in_=node_weight.rearrange("(g p t) -> p g t", p=P, t=PACK))
+        load_weight("self", w_self)
+        load_weight("neigh", w_neigh)
+        load_group(0)
+        load_group(1)
+
+        ident = keep.tile([P, P], F32)
+        make_identity(nc, ident[:])
+        members = keep.tile([P, PACK, 8], F32)
+        nc.vector.tensor_reduce(
+            out=members[:],
+            in_=ident[:].rearrange("q (i t n) -> q t i n", t=PACK, n=FAN),
+            axis=mybir.AxisListType.X,
+            op=ALU.add,
+        )
+        mean_of = keep.tile([P, PACK, 8], BF16)
+        nc.vector.tensor_scalar(out=mean_of[:], in0=members[:], scalar1=1.0 / FAN, scalar2=None, op0=ALU.mult)
+        weight = keep.tile([P, GROUPS * PACK], F32)
+        nc.scalar.activation(out=weight[:], in_=weight_raw[:].rearrange("p g t -> p (g t)"), func=ACT.Copy)
+        y_scales = keep.tile([P, HID], U8, align_bytes=64)
+
+        interleave_weight("self", 0)
+        interleave_weight("self", 1)
+        quantize_weight("self", 0)
+        interleave_weight("neigh", 0)
+        quantize_weight("self", 1)
+        interleave_weight("neigh", 1)
+        quantize_weight("neigh", 0)
+        for a in range(2):
+            turn_x(0, a)
+            copy_x(0, a)
+        for b in range(4):
+            mean_nb(0, b)
+            copy_nb(0, b)
+        quantize_x(0)
+        quantize_weight("neigh", 1)
+        quantize_nb(0)
+        load_group(2)
+        for t in range(PACK):
+            products(0, t)
+
+        for u in range(UNITS):
+            g, h = divmod(u, HALVES)
+            ahead = g + 1 < GROUPS
+            if u == 2:
+                load_group(3)
+                store_y(0)
+                store_y(1)
+            for t in range(PACK):
+                epilogue(u, t)
+                if t == 1 and u > 0:
+                    interleave_y(u - 1)
+                if t == 2 and u > 0:
+                    quantize_y(u - 1)
+                    if h == 0:
+                        store_codes(g - 1, slice(0, HID))
+                    elif not ahead:
+                        store_codes(g, slice(0, HALF))
+                if h == 0:
+                    products(u + 1, t)
+                    if ahead and t == 1:
+                        for a in range(2):
+                            turn_x(g + 1, a)
+                            copy_x(g + 1, a)
+                        mean_nb(g + 1, 0)
+                    if ahead and t == 2:
+                        mean_nb(g + 1, 1)
+                        copy_nb(g + 1, 0)
+                    if ahead and t == 3:
+                        mean_nb(g + 1, 2)
+                        copy_nb(g + 1, 1)
+                        quantize_x(g + 1)
+                elif ahead:
+                    if t == 0:
+                        mean_nb(g + 1, 3)
+                        copy_nb(g + 1, 2)
+                        copy_nb(g + 1, 3)
+                    if t == 1:
+                        quantize_nb(g + 1)
+                        products(u + 1, 0)
+                    if t >= 1:
+                        products(u + 1, t)
+            if u >= 2:
+                store_y(u)
+        interleave_y(UNITS - 1)
+        quantize_y(UNITS - 1)
+        store_codes(GROUPS - 1, slice(HALF, HID))
+        for q in range(4):
+            nc.scalar.dma_start(
+                out=out_2[:, 4 * q : 4 * q + 4, :].bitcast(I32), in_=y_scales[32 * q : 32 * q + 16, :].bitcast(I32)
+            )

@@ -25,6 +25,9 @@ UNITS = GROUPS * HALVES
 CHUNK_NODES = P // FAN
 CHUNKS_PER_LOAD = 8
 CHUNKS_PER_BANK = 4
+RUNS = (1, 2)
+SPLIT = 416
+LAST_SPLIT = 192
 
 
 def tile_graphsage_mean_skip_layer_g2_kernel(
@@ -45,24 +48,34 @@ def tile_graphsage_mean_skip_layer_g2_kernel(
             nc.sync.dma_start(out=raw[:], in_=w.rearrange("(p j) n -> p j n", j=PACK))
             tiles["w_raw", name] = raw
 
-        def load_group(g):
-            rows = slice(g * GROUP, (g + 1) * GROUP)
-            x_raw = stream.tile([P, PACK, F], BF16, name="x_raw%d" % g, tag="x_raw", bufs=2)
-            nc.sync.dma_start(out=x_raw[:], in_=x[rows, :].rearrange("(p t) f -> p t f", t=PACK))
+        def load_x(g):
+            x_raw = stream.tile([P, PACK, F], BF16, name="x_raw", tag="x_raw", bufs=2)
+            rows = x[g * GROUP : (g + 1) * GROUP, :]
+            nc.sync.dma_start(out=x_raw[:], in_=rows.rearrange("(p t) f -> p t f", t=PACK))
             tiles["x_raw", g] = x_raw
+
+        def load_nb(g, a):
+            nb_raw = stream.tile([P, CHUNKS_PER_LOAD, F], BF16, name="nb_raw", tag="raw", bufs=6)
             n_rows = CHUNKS_PER_LOAD * P
-            for a in range(2):
-                nb_raw = stream.tile(
-                    [P, CHUNKS_PER_LOAD, F], BF16, name="nb_raw%d_%d" % (g, a), tag="raw", bufs=6
-                )
-                r0 = (2 * g + a) * n_rows
-                nc.sync.dma_start(
-                    out=nb_raw[:], in_=nb_rows[r0 : r0 + n_rows, :].rearrange("(c q) f -> q c f", q=P)
-                )
-                tiles["nb_raw", g, a] = nb_raw
-            skip_raw = stream.tile([P, PACK, HID], BF16, name="skip%d" % g, tag="skip", bufs=3)
-            nc.sync.dma_start(out=skip_raw[:], in_=skip[rows, :].rearrange("(p t) m -> p t m", t=PACK))
+            r0 = (2 * g + a) * n_rows
+            run = RUNS[a]
+            nc.sync.dma_start(
+                out=nb_raw[:].rearrange("q (c s) f -> q c (s f)", s=run),
+                in_=nb_rows[r0 : r0 + n_rows, :].rearrange("(c q s) f -> q c (s f)", q=P, s=run),
+            )
+            tiles["nb_raw", g, a] = nb_raw
+
+        def load_skip(g):
+            skip_raw = stream.tile([P, PACK, HID], BF16, name="skip_raw", tag="skip", bufs=3)
+            rows = skip[g * GROUP : (g + 1) * GROUP, :]
+            nc.sync.dma_start(out=skip_raw[:], in_=rows.rearrange("(p t) m -> p t m", t=PACK))
             tiles["skip", g] = skip_raw
+
+        def load_step(g):
+            load_x(g)
+            load_skip(g - 1)
+            load_nb(g, 0)
+            load_nb(g, 1)
 
         def quantize(key, staged, tag, bufs):
             codes = stream.tile([P, HALF], U32, name="codes_" + tag, tag="codes_" + tag, bufs=bufs, align_bytes=64)
@@ -73,15 +86,16 @@ def tile_graphsage_mean_skip_layer_g2_kernel(
         def staged_tile(tag, bufs):
             return stream.tile([P, HALF * PACK], BF16, name=tag, tag=tag, bufs=bufs, align_bytes=64)
 
-        def interleave(key, src):
-            staged = staged_tile("staged", 4)
-            nc.vector.tensor_copy(
-                out=staged[:].rearrange("p (m j) -> p m j", j=PACK), in_=src.rearrange("p j m -> p m j")
+        def interleave(copy, staged, src, lo, hi):
+            copy(
+                out=staged[:, PACK * lo : PACK * hi].rearrange("p (c i j) -> p c j i", i=4, j=PACK),
+                in_=src[:, :, lo:hi].rearrange("p j (c i) -> p c j i", i=4),
             )
-            tiles[key] = staged
 
         def interleave_weight(name, h):
-            interleave(("w_staged", name, h), tiles["w_raw", name][:, :, h * HALF : (h + 1) * HALF])
+            tiles["w_staged", name, h] = staged_tile("staged", 4)
+            src = tiles["w_raw", name][:, :, h * HALF : (h + 1) * HALF]
+            interleave(nc.vector.tensor_copy, tiles["w_staged", name, h], src, 0, HALF)
 
         def quantize_weight(name, h):
             quantize(("w", name, h), tiles["w_staged", name, h], "w", 4)
@@ -103,14 +117,21 @@ def tile_graphsage_mean_skip_layer_g2_kernel(
             )
 
         def mean_nb(g, b):
-            bank = psum.tile([P, PACK, PACK, CHUNKS_PER_BANK, 8], F32, name="nb_bank", tag="turn")
+            bank = psum.tile([P, PACK, PACK, 32], F32, name="nb_bank", tag="turn")
             nb_raw = tiles["nb_raw", g, b // 2]
-            for c in range(CHUNKS_PER_BANK):
-                chunk = (b % 2) * CHUNKS_PER_BANK + c
+            run = RUNS[b // 2]
+            width = 8 * run
+            for c in range(CHUNKS_PER_BANK // run):
                 for j in range(PACK):
-                    nc.tensor.matmul(
-                        bank[:, j, :, c, :], lhsT=nb_raw[:, chunk, j:F:PACK], rhs=mean_of[:], start=True, stop=True
-                    )
+                    for s in range(run):
+                        row = (b % 2) * CHUNKS_PER_BANK + c * run + s
+                        nc.tensor.matmul(
+                            bank[:, j, :, c * width : (c + 1) * width],
+                            lhsT=nb_raw[:, row, j:F:PACK],
+                            rhs=mean_of[run][:],
+                            start=(s == 0),
+                            stop=(s == run - 1),
+                        )
             tiles["nb_bank", g, b] = bank
 
         def copy_nb(g, b):
@@ -119,7 +140,7 @@ def tile_graphsage_mean_skip_layer_g2_kernel(
             dst = tiles["nb_staged", g][:].rearrange("k (t p j) -> k t p j", t=PACK, j=PACK)
             nc.scalar.copy(
                 out=dst[:, :, 32 * b : 32 * b + 32, :],
-                in_=tiles["nb_bank", g, b][:].rearrange("k j t c i -> k t (c i) j"),
+                in_=tiles["nb_bank", g, b][:].rearrange("k j t i -> k t i j"),
             )
 
         def quantize_x(g):
@@ -128,8 +149,8 @@ def tile_graphsage_mean_skip_layer_g2_kernel(
         def quantize_nb(g):
             quantize(("act", "neigh", g), tiles["nb_staged", g], "nb", 2)
 
-        def products(u, t):
-            g, h = divmod(u, HALVES)
+        def products(g, s):
+            t, h = divmod(s, HALVES)
             acc = psum.tile([P, HALF], F32, name="acc", tag="acc")
             cols = slice(t * P, (t + 1) * P)
             for i, name in enumerate(("self", "neigh")):
@@ -144,30 +165,32 @@ def tile_graphsage_mean_skip_layer_g2_kernel(
                     start=(i == 0),
                     stop=(i == 1),
                 )
-            tiles["acc", u, t] = acc
+            tiles["acc", g, s] = acc
 
-        def epilogue(u, t):
-            g, h = divmod(u, HALVES)
-            if t == 0:
-                tiles["y", u] = stream.tile([P, PACK, HALF], F32, name="y", tag="y", bufs=UNITS)
-            y = tiles["y", u]
+        def relu_skip(g, s):
+            t, h = divmod(s, HALVES)
+            if s == 0:
+                tiles["y", g] = stream.tile([P, PACK, HID], F32, name="y", tag="y", bufs=GROUPS)
+            cols = slice(h * HALF, (h + 1) * HALF)
             nc.vector.scalar_tensor_tensor(
-                out=y[:, t, :],
-                in0=tiles["acc", u, t][:],
+                out=tiles["y", g][:, t, cols],
+                in0=tiles["acc", g, s][:],
                 scalar=0.0,
-                in1=tiles["skip", g][:, t, h * HALF : (h + 1) * HALF],
+                in1=tiles["skip", g][:, t, cols],
                 op0=ALU.max,
                 op1=ALU.add,
             )
-            nc.scalar.activation(
-                out=y[:, t, :], in_=y[:, t, :], func=ACT.Copy, scale=weight[:, g * PACK + t : g * PACK + t + 1]
-            )
 
-        def interleave_y(u):
-            interleave(("y_staged", u), tiles["y", u][:])
+        def weigh(g, t, cols):
+            y = tiles["y", g][:, t, cols]
+            nc.scalar.activation(out=y, in_=y, func=ACT.Copy, scale=weight[:, g * PACK + t : g * PACK + t + 1])
 
-        def quantize_y(u):
-            g, h = divmod(u, HALVES)
+        def interleave_y(g, h, copy, lo, hi):
+            if ("y_staged", g, h) not in tiles:
+                tiles["y_staged", g, h] = staged_tile("staged", 4)
+            interleave(copy, tiles["y_staged", g, h], tiles["y", g][:, :, h * HALF : (h + 1) * HALF], lo, hi)
+
+        def quantize_y(g, h):
             if h == 0:
                 tiles["y_codes", g] = stream.tile(
                     [P, HID], U32, name="y_codes", tag="y_codes", bufs=GROUPS, align_bytes=64
@@ -176,13 +199,12 @@ def tile_graphsage_mean_skip_layer_g2_kernel(
             nc.vector.quantize_mx(
                 out=tiles["y_codes", g][:, cols].bitcast(FP8X4),
                 scales=y_scales[PACK * g : P, cols],
-                in_=tiles["y_staged", u][:],
+                in_=tiles["y_staged", g, h][:],
             )
 
-        def store_y(u):
-            g, h = divmod(u, HALVES)
-            dst = out_0[g * GROUP : (g + 1) * GROUP, h * HALF : (h + 1) * HALF]
-            nc.sync.dma_start(out=dst.rearrange("(p t) m -> p t m", t=PACK), in_=tiles["y", u][:])
+        def store_y(g, slots):
+            dst = out_0[g * GROUP : (g + 1) * GROUP, :].rearrange("(p t) m -> p t m", t=PACK)
+            nc.sync.dma_start(out=dst[:, slots, :], in_=tiles["y", g][:, slots, :])
 
         def store_codes(g, cols):
             dst = out_1[g].rearrange("p m t -> p (m t)").bitcast(I32)
@@ -191,91 +213,126 @@ def tile_graphsage_mean_skip_layer_g2_kernel(
         weight_raw = keep.tile([P, GROUPS, PACK], BF16)
         nc.scalar.dma_start(out=weight_raw[:], in_=node_weight.rearrange("(g p t) -> p g t", p=P, t=PACK))
         load_weight("self", w_self)
+        load_x(0)
+        load_nb(0, 0)
         load_weight("neigh", w_neigh)
-        load_group(0)
-        load_group(1)
+        load_nb(0, 1)
+        load_step(1)
 
         ident = keep.tile([P, P], F32)
         make_identity(nc, ident[:])
-        members = keep.tile([P, PACK, 8], F32)
-        nc.vector.tensor_reduce(
-            out=members[:],
-            in_=ident[:].rearrange("q (i t n) -> q t i n", t=PACK, n=FAN),
-            axis=mybir.AxisListType.X,
-            op=ALU.add,
-        )
-        mean_of = keep.tile([P, PACK, 8], BF16)
-        nc.vector.tensor_scalar(out=mean_of[:], in0=members[:], scalar1=1.0 / FAN, scalar2=None, op0=ALU.mult)
+        mean_of = {}
+        for run in sorted(set(RUNS)):
+            members = keep.tile([P, PACK, 8 * run], F32, name="members%d" % run)
+            nc.vector.tensor_reduce(
+                out=members[:],
+                in_=ident[:].rearrange("q (i t n) -> q t i n", t=PACK, n=FAN // run),
+                axis=mybir.AxisListType.X,
+                op=ALU.add,
+            )
+            mean_of[run] = keep.tile([P, PACK, 8 * run], BF16, name="mean_of%d" % run)
+            nc.vector.tensor_scalar(
+                out=mean_of[run][:], in0=members[:], scalar1=1.0 / FAN, scalar2=None, op0=ALU.mult
+            )
         weight = keep.tile([P, GROUPS * PACK], F32)
         nc.scalar.activation(out=weight[:], in_=weight_raw[:].rearrange("p g t -> p (g t)"), func=ACT.Copy)
         y_scales = keep.tile([P, HID], U8, align_bytes=64)
 
+        def turn_and_copy_x(g):
+            for a in range(2):
+                turn_x(g, a)
+            for a in range(2):
+                copy_x(g, a)
+
+        def mean_and_copy_nb(g, b):
+            mean_nb(g, b)
+            copy_nb(g, b)
+
         interleave_weight("self", 0)
         interleave_weight("self", 1)
+        turn_and_copy_x(0)
         quantize_weight("self", 0)
-        interleave_weight("neigh", 0)
         quantize_weight("self", 1)
-        interleave_weight("neigh", 1)
-        quantize_weight("neigh", 0)
-        for a in range(2):
-            turn_x(0, a)
-            copy_x(0, a)
-        for b in range(4):
-            mean_nb(0, b)
-            copy_nb(0, b)
+        mean_and_copy_nb(0, 0)
+        mean_and_copy_nb(0, 1)
         quantize_x(0)
-        quantize_weight("neigh", 1)
+        interleave_weight("neigh", 0)
+        interleave_weight("neigh", 1)
+        mean_and_copy_nb(0, 2)
+        mean_and_copy_nb(0, 3)
+        quantize_weight("neigh", 0)
         quantize_nb(0)
-        load_group(2)
-        for t in range(PACK):
-            products(0, t)
+        quantize_weight("neigh", 1)
+        load_step(2)
 
-        for u in range(UNITS):
-            g, h = divmod(u, HALVES)
+        whole = slice(0, HID)
+        for g in range(GROUPS):
+            behind = g > 0
             ahead = g + 1 < GROUPS
-            if u == 2:
-                load_group(3)
-                store_y(0)
-                store_y(1)
-            for t in range(PACK):
-                epilogue(u, t)
-                if t == 1 and u > 0:
-                    interleave_y(u - 1)
-                if t == 2 and u > 0:
-                    quantize_y(u - 1)
-                    if h == 0:
-                        store_codes(g - 1, slice(0, HID))
-                    elif not ahead:
-                        store_codes(g, slice(0, HALF))
-                if h == 0:
-                    products(u + 1, t)
-                    if ahead and t == 1:
-                        for a in range(2):
-                            turn_x(g + 1, a)
-                            copy_x(g + 1, a)
-                        mean_nb(g + 1, 0)
-                    if ahead and t == 2:
-                        mean_nb(g + 1, 1)
-                        copy_nb(g + 1, 0)
-                    if ahead and t == 3:
-                        mean_nb(g + 1, 2)
-                        copy_nb(g + 1, 1)
-                        quantize_x(g + 1)
-                elif ahead:
-                    if t == 0:
-                        mean_nb(g + 1, 3)
-                        copy_nb(g + 1, 2)
-                        copy_nb(g + 1, 3)
-                    if t == 1:
-                        quantize_nb(g + 1)
-                        products(u + 1, 0)
-                    if t >= 1:
-                        products(u + 1, t)
-            if u >= 2:
-                store_y(u)
-        interleave_y(UNITS - 1)
-        quantize_y(UNITS - 1)
-        store_codes(GROUPS - 1, slice(HALF, HID))
+            if ahead:
+                turn_and_copy_x(g + 1)
+            if g == 0:
+                load_step(3)
+            for s in range(4):
+                products(g, s)
+            relu_skip(g, 0)
+            products(g, 4)
+            relu_skip(g, 1)
+            if behind:
+                for h in range(HALVES):
+                    interleave_y(g - 1, h, nc.scalar.copy, SPLIT, HALF)
+            relu_skip(g, 2)
+            if ahead:
+                quantize_x(g + 1)
+                mean_and_copy_nb(g + 1, 0)
+            if behind:
+                interleave_y(g - 1, 0, nc.vector.tensor_copy, 0, SPLIT)
+            weigh(g, 0, whole)
+            if ahead:
+                mean_and_copy_nb(g + 1, 1)
+            if behind:
+                interleave_y(g - 1, 1, nc.vector.tensor_copy, 0, SPLIT)
+            if ahead:
+                mean_and_copy_nb(g + 1, 2)
+            relu_skip(g, 3)
+            if behind:
+                for h in range(HALVES):
+                    quantize_y(g - 1, h)
+                store_codes(g - 1, whole)
+            if ahead:
+                mean_and_copy_nb(g + 1, 3)
+            for s in range(5, 8):
+                products(g, s)
+            relu_skip(g, 4)
+            weigh(g, 1, whole)
+            if g >= 2:
+                store_y(g, slice(0, 2))
+            relu_skip(g, 5)
+            if ahead:
+                quantize_nb(g + 1)
+                relu_skip(g, 6)
+                weigh(g, 2, whole)
+                relu_skip(g, 7)
+                weigh(g, 3, whole)
+                if g == 0:
+                    load_skip(GROUPS - 1)
+                store_y(g, slice(2 if g >= 2 else 0, PACK))
+            else:
+                weigh(g, 2, whole)
+                store_y(g, slice(2, 3))
+                relu_skip(g, 6)
+                weigh(g, 3, slice(0, HALF))
+                relu_skip(g, 7)
+                weigh(g, 3, slice(HALF, HID))
+                store_y(g, slice(3, 4))
+        g = GROUPS - 1
+        interleave_y(g, 0, nc.vector.tensor_copy, 0, HALF)
+        interleave_y(g, 1, nc.scalar.copy, LAST_SPLIT, HALF)
+        interleave_y(g, 1, nc.vector.tensor_copy, 0, LAST_SPLIT)
+        quantize_y(g, 0)
+        store_codes(g, slice(0, HALF))
+        quantize_y(g, 1)
+        store_codes(g, slice(HALF, HID))
         for q in range(4):
             nc.scalar.dma_start(
                 out=out_2[:, 4 * q : 4 * q + 4, :].bitcast(I32), in_=y_scales[32 * q : 32 * q + 16, :].bitcast(I32)

@@ -25,8 +25,9 @@ UNITS = GROUPS * HALVES
 CHUNK_NODES = P // FAN
 CHUNKS_PER_LOAD = 8
 CHUNKS_PER_BANK = 4
-RUNS = (1, 2)
-SPLIT = 416
+NB_ROWS = 16
+RUNS = ((1, 2), (1, 2), (1, 1), (2, 2))
+SPLIT = 384
 LAST_SPLIT = 192
 
 
@@ -44,38 +45,29 @@ def tile_graphsage_mean_skip_layer_g2_kernel(
         tiles = {}
 
         def load_weight(name, w):
-            raw = stream.tile([P, PACK, HID], BF16, name="raw_" + name, tag="raw", bufs=6)
+            raw = stream.tile([P, PACK, HID], BF16, name="raw_" + name, tag="wide", bufs=4)
             nc.sync.dma_start(out=raw[:], in_=w.rearrange("(p j) n -> p j n", j=PACK))
             tiles["w_raw", name] = raw
 
-        def load_x(g):
-            x_raw = stream.tile([P, PACK, F], BF16, name="x_raw", tag="x_raw", bufs=2)
-            rows = x[g * GROUP : (g + 1) * GROUP, :]
-            nc.sync.dma_start(out=x_raw[:], in_=rows.rearrange("(p t) f -> p t f", t=PACK))
-            tiles["x_raw", g] = x_raw
+        def load_x(groups):
+            rows = x.rearrange("(g p t) f -> p g (t f)", p=P, t=PACK)
+            nc.sync.dma_start(out=x_raw[:, groups, :], in_=rows[:, groups, :])
 
-        def load_nb(g, a):
-            nb_raw = stream.tile([P, CHUNKS_PER_LOAD, F], BF16, name="nb_raw", tag="raw", bufs=6)
-            n_rows = CHUNKS_PER_LOAD * P
-            r0 = (2 * g + a) * n_rows
-            run = RUNS[a]
+        def load_nb(g, rows):
+            if rows.start == 0:
+                tiles["nb_raw", g] = stream.tile([P, NB_ROWS, F], BF16, name="nb_raw", tag="nb_raw", bufs=3)
+            run = RUNS[g][rows.start // (NB_ROWS // 2)]
+            src = nb_rows[(g * NB_ROWS + rows.start) * P : (g * NB_ROWS + rows.stop) * P, :]
             nc.sync.dma_start(
-                out=nb_raw[:].rearrange("q (c s) f -> q c (s f)", s=run),
-                in_=nb_rows[r0 : r0 + n_rows, :].rearrange("(c q s) f -> q c (s f)", q=P, s=run),
+                out=tiles["nb_raw", g][:, rows, :].rearrange("q (c s) f -> q c (s f)", s=run),
+                in_=src.rearrange("(c q s) f -> q c (s f)", q=P, s=run),
             )
-            tiles["nb_raw", g, a] = nb_raw
 
         def load_skip(g):
-            skip_raw = stream.tile([P, PACK, HID], BF16, name="skip_raw", tag="skip", bufs=3)
+            skip_raw = stream.tile([P, PACK, HID], BF16, name="skip_raw", tag="wide", bufs=4)
             rows = skip[g * GROUP : (g + 1) * GROUP, :]
             nc.sync.dma_start(out=skip_raw[:], in_=rows.rearrange("(p t) m -> p t m", t=PACK))
             tiles["skip", g] = skip_raw
-
-        def load_step(g):
-            load_x(g)
-            load_skip(g - 1)
-            load_nb(g, 0)
-            load_nb(g, 1)
 
         def quantize(key, staged, tag, bufs):
             codes = stream.tile([P, HALF], U32, name="codes_" + tag, tag="codes_" + tag, bufs=bufs, align_bytes=64)
@@ -103,7 +95,7 @@ def tile_graphsage_mean_skip_layer_g2_kernel(
         def turn_x(g, a):
             bank = psum.tile([P, 2, 2, P], F32, name="x_bank", tag="turn")
             for s in range(2):
-                words = tiles["x_raw", g][:, 2 * a + s, :].bitcast(F32)
+                words = x_raw[:, g, (2 * a + s) * F : (2 * a + s + 1) * F].bitcast(F32)
                 for u in range(2):
                     nc.tensor.transpose(bank[:, s, u, :], words[:, u : F // 2 : 2], ident[:])
             tiles["x_bank", g, a] = bank
@@ -118,13 +110,13 @@ def tile_graphsage_mean_skip_layer_g2_kernel(
 
         def mean_nb(g, b):
             bank = psum.tile([P, PACK, PACK, 32], F32, name="nb_bank", tag="turn")
-            nb_raw = tiles["nb_raw", g, b // 2]
-            run = RUNS[b // 2]
+            nb_raw = tiles["nb_raw", g]
+            run = RUNS[g][b // 2]
             width = 8 * run
             for c in range(CHUNKS_PER_BANK // run):
                 for j in range(PACK):
                     for s in range(run):
-                        row = (b % 2) * CHUNKS_PER_BANK + c * run + s
+                        row = b * CHUNKS_PER_BANK + c * run + s
                         nc.tensor.matmul(
                             bank[:, j, :, c * width : (c + 1) * width],
                             lhsT=nb_raw[:, row, j:F:PACK],
@@ -169,11 +161,9 @@ def tile_graphsage_mean_skip_layer_g2_kernel(
 
         def relu_skip(g, s):
             t, h = divmod(s, HALVES)
-            if s == 0:
-                tiles["y", g] = stream.tile([P, PACK, HID], F32, name="y", tag="y", bufs=GROUPS)
             cols = slice(h * HALF, (h + 1) * HALF)
             nc.vector.scalar_tensor_tensor(
-                out=tiles["y", g][:, t, cols],
+                out=y_all[:, g, t, cols],
                 in0=tiles["acc", g, s][:],
                 scalar=0.0,
                 in1=tiles["skip", g][:, t, cols],
@@ -182,47 +172,55 @@ def tile_graphsage_mean_skip_layer_g2_kernel(
             )
 
         def weigh(g, t, cols):
-            y = tiles["y", g][:, t, cols]
-            nc.scalar.activation(out=y, in_=y, func=ACT.Copy, scale=weight[:, g * PACK + t : g * PACK + t + 1])
+            y = y_all[:, g, t, cols]
+            nc.scalar.activation(out=y, in_=y, func=ACT.Copy, scale=weight[:, t, g : g + 1])
 
         def interleave_y(g, h, copy, lo, hi):
             if ("y_staged", g, h) not in tiles:
                 tiles["y_staged", g, h] = staged_tile("staged", 4)
-            interleave(copy, tiles["y_staged", g, h], tiles["y", g][:, :, h * HALF : (h + 1) * HALF], lo, hi)
+            interleave(copy, tiles["y_staged", g, h], y_all[:, g, :, h * HALF : (h + 1) * HALF], lo, hi)
 
         def quantize_y(g, h):
-            if h == 0:
-                tiles["y_codes", g] = stream.tile(
-                    [P, HID], U32, name="y_codes", tag="y_codes", bufs=GROUPS, align_bytes=64
-                )
             cols = slice(h * HALF, (h + 1) * HALF)
             nc.vector.quantize_mx(
-                out=tiles["y_codes", g][:, cols].bitcast(FP8X4),
+                out=y_codes[:, g, cols].bitcast(FP8X4),
                 scales=y_scales[PACK * g : P, cols],
                 in_=tiles["y_staged", g, h][:],
             )
 
-        def store_y(g, slots):
-            dst = out_0[g * GROUP : (g + 1) * GROUP, :].rearrange("(p t) m -> p t m", t=PACK)
-            nc.sync.dma_start(out=dst[:, slots, :], in_=tiles["y", g][:, slots, :])
+        def store_y(groups, slots):
+            dst = out_0.rearrange("(g p t) m -> p g t m", p=P, t=PACK)
+            nc.sync.dma_start(out=dst[:, groups, slots, :], in_=y_all[:, groups, slots, :])
 
-        def store_codes(g, cols):
-            dst = out_1[g].rearrange("p m t -> p (m t)").bitcast(I32)
-            nc.sync.dma_start(out=dst[:, cols], in_=tiles["y_codes", g][:, cols].bitcast(I32))
+        def store_codes(groups, cols):
+            dst = out_1.rearrange("g p m t -> p g (m t)").bitcast(I32)
+            nc.sync.dma_start(out=dst[:, groups, cols], in_=y_codes[:, groups, cols].bitcast(I32))
 
-        weight_raw = keep.tile([P, GROUPS, PACK], BF16)
-        nc.scalar.dma_start(out=weight_raw[:], in_=node_weight.rearrange("(g p t) -> p g t", p=P, t=PACK))
+        weight_raw = keep.tile([P, GROUP], BF16, name="weight_raw")
+        nc.gpsimd.memset(weight_raw[:], 0.0)
+        nc.scalar.dma_start(out=weight_raw[0:GROUPS, :], in_=node_weight.rearrange("(g v) -> g v", g=GROUPS))
+        x_raw = keep.tile([P, GROUPS, PACK * F], BF16, name="x_raw")
+        y_all = keep.tile([P, GROUPS, PACK, HID], F32, name="y")
+        y_codes = keep.tile([P, GROUPS, HID], U32, align_bytes=64, name="y_codes")
+        first, second = slice(0, NB_ROWS // 2), slice(NB_ROWS // 2, NB_ROWS)
         load_weight("self", w_self)
-        load_x(0)
-        load_nb(0, 0)
+        load_x(slice(0, 1))
+        load_nb(0, first)
         load_weight("neigh", w_neigh)
-        load_nb(0, 1)
-        load_step(1)
+        load_nb(0, second)
+        load_x(slice(1, 2))
+        load_skip(0)
+        load_nb(1, first)
+        load_nb(1, second)
+        load_x(slice(2, 4))
+        load_skip(1)
+        load_nb(2, first)
+        load_nb(2, second)
 
         ident = keep.tile([P, P], F32)
         make_identity(nc, ident[:])
         mean_of = {}
-        for run in sorted(set(RUNS)):
+        for run in (1, 2):
             members = keep.tile([P, PACK, 8 * run], F32, name="members%d" % run)
             nc.vector.tensor_reduce(
                 out=members[:],
@@ -234,8 +232,8 @@ def tile_graphsage_mean_skip_layer_g2_kernel(
             nc.vector.tensor_scalar(
                 out=mean_of[run][:], in0=members[:], scalar1=1.0 / FAN, scalar2=None, op0=ALU.mult
             )
-        weight = keep.tile([P, GROUPS * PACK], F32)
-        nc.scalar.activation(out=weight[:], in_=weight_raw[:].rearrange("p g t -> p (g t)"), func=ACT.Copy)
+        ident_bf = keep.tile([P, P], BF16, name="ident_bf")
+        make_identity(nc, ident_bf[:])
         y_scales = keep.tile([P, HID], U8, align_bytes=64)
 
         def turn_and_copy_x(g):
@@ -263,7 +261,14 @@ def tile_graphsage_mean_skip_layer_g2_kernel(
         quantize_weight("neigh", 0)
         quantize_nb(0)
         quantize_weight("neigh", 1)
-        load_step(2)
+        weight_bank = psum.tile([P, PACK, P], BF16, name="weight_bank", tag="turn")
+        for t in range(PACK):
+            nc.tensor.transpose(weight_bank[:, t, :], weight_raw[:, t:GROUP:PACK], ident_bf[:])
+        weight = keep.tile([P, PACK, GROUPS], F32, name="weight")
+        nc.scalar.activation(out=weight[:], in_=weight_bank[:, :, 0:GROUPS], func=ACT.Copy)
+        load_skip(2)
+        load_nb(3, slice(0, NB_ROWS))
+        load_skip(3)
 
         whole = slice(0, HID)
         for g in range(GROUPS):
@@ -271,8 +276,6 @@ def tile_graphsage_mean_skip_layer_g2_kernel(
             ahead = g + 1 < GROUPS
             if ahead:
                 turn_and_copy_x(g + 1)
-            if g == 0:
-                load_step(3)
             for s in range(4):
                 products(g, s)
             relu_skip(g, 0)
@@ -298,14 +301,15 @@ def tile_graphsage_mean_skip_layer_g2_kernel(
             if behind:
                 for h in range(HALVES):
                     quantize_y(g - 1, h)
-                store_codes(g - 1, whole)
+                if g >= 2:
+                    store_codes(slice(0, 2) if ahead else slice(2, 3), whole)
             if ahead:
                 mean_and_copy_nb(g + 1, 3)
             for s in range(5, 8):
                 products(g, s)
             relu_skip(g, 4)
             weigh(g, 1, whole)
-            if g >= 2:
+            if not ahead:
                 store_y(g, slice(0, 2))
             relu_skip(g, 5)
             if ahead:
@@ -314,25 +318,21 @@ def tile_graphsage_mean_skip_layer_g2_kernel(
                 weigh(g, 2, whole)
                 relu_skip(g, 7)
                 weigh(g, 3, whole)
-                if g == 0:
-                    load_skip(GROUPS - 1)
-                store_y(g, slice(2 if g >= 2 else 0, PACK))
+                store_y(g, slice(0, PACK))
             else:
                 weigh(g, 2, whole)
-                store_y(g, slice(2, 3))
                 relu_skip(g, 6)
                 weigh(g, 3, slice(0, HALF))
                 relu_skip(g, 7)
                 weigh(g, 3, slice(HALF, HID))
-                store_y(g, slice(3, 4))
+                store_y(g, slice(2, 4))
         g = GROUPS - 1
         interleave_y(g, 0, nc.vector.tensor_copy, 0, HALF)
         interleave_y(g, 1, nc.scalar.copy, LAST_SPLIT, HALF)
         interleave_y(g, 1, nc.vector.tensor_copy, 0, LAST_SPLIT)
         quantize_y(g, 0)
-        store_codes(g, slice(0, HALF))
         quantize_y(g, 1)
-        store_codes(g, slice(HALF, HID))
+        store_codes(g, whole)
         for q in range(4):
             nc.scalar.dma_start(
                 out=out_2[:, 4 * q : 4 * q + 4, :].bitcast(I32), in_=y_scales[32 * q : 32 * q + 16, :].bitcast(I32)

@@ -21,14 +21,14 @@ GROUP = P * PACK
 GROUPS = NODES // GROUP
 HALF = 512
 HALVES = HID // HALF
-UNITS = GROUPS * HALVES
-CHUNK_NODES = P // FAN
-CHUNKS_PER_LOAD = 8
-CHUNKS_PER_BANK = 4
-NB_ROWS = 16
-RUNS = ((1, 2), (1, 2), (1, 1), (2, 2))
+NB_ROWS = GROUP * FAN // P
+RUN = 2
+CHUNK = P * RUN // FAN
+BANKS = GROUP // P
+QUADRANTS = 4
 SPLIT = 384
-LAST_SPLIT = 192
+LAST_ROUND_SPLIT = 320
+TAIL_SPLITS = (448, 256)
 
 
 def tile_graphsage_mean_skip_layer_g2_kernel(
@@ -43,37 +43,45 @@ def tile_graphsage_mean_skip_layer_g2_kernel(
 
         nb_rows = neighbours.rearrange("v n f -> (v n) f")
         tiles = {}
+        first, second, both = slice(0, NB_ROWS // 2), slice(NB_ROWS // 2, NB_ROWS), slice(0, NB_ROWS)
+        whole = slice(0, HID)
+
+        def half(h):
+            return slice(h * HALF, (h + 1) * HALF)
+
+
+        def wide_tile():
+            return stream.tile([P, PACK, HID], BF16, name="wide", tag="wide", bufs=4)
 
         def load_weight(name, w):
-            raw = stream.tile([P, PACK, HID], BF16, name="raw_" + name, tag="wide", bufs=4)
-            nc.sync.dma_start(out=raw[:], in_=w.rearrange("(p j) n -> p j n", j=PACK))
-            tiles["w_raw", name] = raw
+            tiles["w_raw", name] = wide_tile()
+            nc.sync.dma_start(out=tiles["w_raw", name][:], in_=w.rearrange("(p j) n -> p j n", j=PACK))
+
+        def load_skip(g):
+            tiles["skip", g] = wide_tile()
+            rows = skip[g * GROUP : (g + 1) * GROUP, :]
+            nc.sync.dma_start(out=tiles["skip", g][:], in_=rows.rearrange("(p t) m -> p t m", t=PACK))
 
         def load_x(groups):
             rows = x.rearrange("(g p t) f -> p g (t f)", p=P, t=PACK)
             nc.sync.dma_start(out=x_raw[:, groups, :], in_=rows[:, groups, :])
 
-        def load_nb(g, rows):
-            if rows.start == 0:
+        def nb_tile(g):
+            if ("nb_raw", g) not in tiles:
                 tiles["nb_raw", g] = stream.tile([P, NB_ROWS, F], BF16, name="nb_raw", tag="nb_raw", bufs=3)
-            run = RUNS[g][rows.start // (NB_ROWS // 2)]
+            return tiles["nb_raw", g]
+
+        def load_nb_by_node(rows):
+            src = nb_rows[0 : NB_ROWS * P, :].rearrange("(p r) f -> p r f", p=P)
+            nc.sync.dma_start(out=nb_tile(0)[:, rows, :], in_=src[:, rows, :])
+
+        def load_nb_spread(g, rows):
             src = nb_rows[(g * NB_ROWS + rows.start) * P : (g * NB_ROWS + rows.stop) * P, :]
             nc.sync.dma_start(
-                out=tiles["nb_raw", g][:, rows, :].rearrange("q (c s) f -> q c (s f)", s=run),
-                in_=src.rearrange("(c q s) f -> q c (s f)", q=P, s=run),
+                out=nb_tile(g)[:, rows, :].rearrange("q (c s) f -> q c (s f)", s=RUN),
+                in_=src.rearrange("(c q s) f -> q c (s f)", q=P, s=RUN),
             )
 
-        def load_skip(g):
-            skip_raw = stream.tile([P, PACK, HID], BF16, name="skip_raw", tag="wide", bufs=4)
-            rows = skip[g * GROUP : (g + 1) * GROUP, :]
-            nc.sync.dma_start(out=skip_raw[:], in_=rows.rearrange("(p t) m -> p t m", t=PACK))
-            tiles["skip", g] = skip_raw
-
-        def quantize(key, staged, tag, bufs):
-            codes = stream.tile([P, HALF], U32, name="codes_" + tag, tag="codes_" + tag, bufs=bufs, align_bytes=64)
-            scales = stream.tile([P, HALF], U8, name="scales_" + tag, tag="scales_" + tag, bufs=bufs, align_bytes=64)
-            nc.vector.quantize_mx(out=codes[:].bitcast(FP8X4), scales=scales[:], in_=staged[:])
-            tiles[key] = (codes, scales)
 
         def staged_tile(tag, bufs):
             return stream.tile([P, HALF * PACK], BF16, name=tag, tag=tag, bufs=bufs, align_bytes=64)
@@ -84,45 +92,64 @@ def tile_graphsage_mean_skip_layer_g2_kernel(
                 in_=src[:, :, lo:hi].rearrange("p j (c i) -> p c j i", i=4),
             )
 
-        def interleave_weight(name, h):
+        def quantize(key, staged, tag, bufs):
+            codes = stream.tile([P, HALF], U32, name="codes_" + tag, tag="codes_" + tag, bufs=bufs, align_bytes=64)
+            scales = stream.tile([P, HALF], U8, name="scales_" + tag, tag="scales_" + tag, bufs=bufs, align_bytes=64)
+            nc.vector.quantize_mx(out=codes[:].bitcast(FP8X4), scales=scales[:], in_=staged[:])
+            tiles[key] = (codes, scales)
+
+        def interleave_weight(name, h, copy):
             tiles["w_staged", name, h] = staged_tile("staged", 4)
-            src = tiles["w_raw", name][:, :, h * HALF : (h + 1) * HALF]
-            interleave(nc.vector.tensor_copy, tiles["w_staged", name, h], src, 0, HALF)
+            interleave(copy, tiles["w_staged", name, h], tiles["w_raw", name][:, :, half(h)], 0, HALF)
 
         def quantize_weight(name, h):
-            quantize(("w", name, h), tiles["w_staged", name, h], "w", 4)
+            quantize(("w", name, h), tiles["w_staged", name, h], "w", 2 * HALVES)
 
-        def turn_x(g, a):
-            bank = psum.tile([P, 2, 2, P], F32, name="x_bank", tag="turn")
-            for s in range(2):
-                words = x_raw[:, g, (2 * a + s) * F : (2 * a + s + 1) * F].bitcast(F32)
-                for u in range(2):
-                    nc.tensor.transpose(bank[:, s, u, :], words[:, u : F // 2 : 2], ident[:])
-            tiles["x_bank", g, a] = bank
+        def turn(rows):
+            banks = []
+            for a in range(2):
+                bank = psum.tile([P, 2, 2, P], F32, name="turned", tag="turn")
+                for s in range(2):
+                    words = rows[:, (2 * a + s) * F : (2 * a + s + 1) * F].bitcast(F32)
+                    for u in range(2):
+                        nc.tensor.transpose(bank[:, s, u, :], words[:, u : F // 2 : 2], ident[:])
+                banks.append(bank)
+            return banks
 
-        def copy_x(g, a):
-            if a == 0:
-                tiles["x_staged", g] = staged_tile("x_staged", 2)
-            dst = tiles["x_staged", g][:].bitcast(F32).rearrange("k (t p u) -> k t p u", t=PACK, u=2)
-            nc.scalar.copy(
-                out=dst[:, 2 * a : 2 * a + 2, :, :], in_=tiles["x_bank", g, a][:].rearrange("k s u p -> k s p u")
+        def copy_turned(key, tag, banks):
+            tiles[key] = staged_tile(tag, 2)
+            dst = tiles[key][:].bitcast(F32).rearrange("k (t p u) -> k t p u", t=PACK, u=2)
+            for a, bank in enumerate(banks):
+                nc.scalar.copy(out=dst[:, 2 * a : 2 * a + 2, :, :], in_=bank[:].rearrange("k s u p -> k s p u"))
+
+        def add_pairs(a):
+            rows = tiles["nb_raw", 0][:, a * 8 : (a + 1) * 8, :].rearrange("p (r e) f -> p r e f", e=2)
+            nc.vector.tensor_tensor(
+                out=pair_sums[:, a * 4 : (a + 1) * 4, :], in0=rows[:, :, 0, :], in1=rows[:, :, 1, :], op=ALU.add
             )
 
+        def add_pair_sums(a):
+            pairs = pair_sums[:, a * 4 : (a + 1) * 4, :].rearrange("p (t e) f -> p t e f", e=2)
+            dst = nb_mean[:, a * 2 * F : (a + 1) * 2 * F].rearrange("p (t f) -> p t f", f=F)
+            nc.vector.tensor_tensor(out=dst, in0=pairs[:, :, 0, :], in1=pairs[:, :, 1, :], op=ALU.add)
+
+        def divide_sums(a):
+            sums = nb_mean[:, a * 2 * F : (a + 1) * 2 * F]
+            nc.vector.tensor_scalar(out=sums, in0=sums, scalar1=1.0 / FAN, scalar2=None, op0=ALU.mult)
+
         def mean_nb(g, b):
-            bank = psum.tile([P, PACK, PACK, 32], F32, name="nb_bank", tag="turn")
-            nb_raw = tiles["nb_raw", g]
-            run = RUNS[g][b // 2]
-            width = 8 * run
-            for c in range(CHUNKS_PER_BANK // run):
+            bank = psum.tile([P, PACK, PACK, P // PACK], F32, name="nb_bank", tag="turn")
+            width = CHUNK // PACK
+            for c in range(P // CHUNK):
                 for j in range(PACK):
-                    for s in range(run):
-                        row = b * CHUNKS_PER_BANK + c * run + s
+                    for s in range(RUN):
+                        row = b * FAN + c * RUN + s
                         nc.tensor.matmul(
                             bank[:, j, :, c * width : (c + 1) * width],
-                            lhsT=nb_raw[:, row, j:F:PACK],
-                            rhs=mean_of[run][:],
+                            lhsT=tiles["nb_raw", g][:, row, j:F:PACK],
+                            rhs=mean_of[:],
                             start=(s == 0),
-                            stop=(s == run - 1),
+                            stop=(s == RUN - 1),
                         )
             tiles["nb_bank", g, b] = bank
 
@@ -135,38 +162,42 @@ def tile_graphsage_mean_skip_layer_g2_kernel(
                 in_=tiles["nb_bank", g, b][:].rearrange("k j t i -> k t i j"),
             )
 
+        def mean_and_copy_nb(g, b):
+            mean_nb(g, b)
+            copy_nb(g, b)
+
         def quantize_x(g):
-            quantize(("act", "self", g), tiles["x_staged", g], "x", 2)
+            quantize(("nodes", "self", g), tiles["x_staged", g], "x", 2)
 
         def quantize_nb(g):
-            quantize(("act", "neigh", g), tiles["nb_staged", g], "nb", 2)
+            quantize(("nodes", "neigh", g), tiles["nb_staged", g], "nb", 2)
 
-        def products(g, s):
-            t, h = divmod(s, HALVES)
+
+        def products(g, step):
+            t, h = divmod(step, HALVES)
             acc = psum.tile([P, HALF], F32, name="acc", tag="acc")
             cols = slice(t * P, (t + 1) * P)
             for i, name in enumerate(("self", "neigh")):
-                a_codes, a_scales = tiles["act", name, g]
+                node_codes, node_scales = tiles["nodes", name, g]
                 w_codes, w_scales = tiles["w", name, h]
                 nc.tensor.matmul_mx(
                     out=acc[:],
-                    lhsT=a_codes[:, cols].bitcast(FP8X4),
-                    lhsT_scale=a_scales[:, cols],
+                    lhsT=node_codes[:, cols].bitcast(FP8X4),
+                    lhsT_scale=node_scales[:, cols],
                     rhs=w_codes[:].bitcast(FP8X4),
                     rhs_scale=w_scales[:],
                     start=(i == 0),
                     stop=(i == 1),
                 )
-            tiles["acc", g, s] = acc
+            tiles["acc", g, step] = acc
 
-        def relu_skip(g, s):
-            t, h = divmod(s, HALVES)
-            cols = slice(h * HALF, (h + 1) * HALF)
+        def relu_skip(g, step):
+            t, h = divmod(step, HALVES)
             nc.vector.scalar_tensor_tensor(
-                out=y_all[:, g, t, cols],
-                in0=tiles["acc", g, s][:],
+                out=y_all[:, g, t, half(h)],
+                in0=tiles["acc", g, step][:],
                 scalar=0.0,
-                in1=tiles["skip", g][:, t, cols],
+                in1=tiles["skip", g][:, t, half(h)],
                 op0=ALU.max,
                 op1=ALU.add,
             )
@@ -178,141 +209,162 @@ def tile_graphsage_mean_skip_layer_g2_kernel(
         def interleave_y(g, h, copy, lo, hi):
             if ("y_staged", g, h) not in tiles:
                 tiles["y_staged", g, h] = staged_tile("staged", 4)
-            interleave(copy, tiles["y_staged", g, h], y_all[:, g, :, h * HALF : (h + 1) * HALF], lo, hi)
+            interleave(copy, tiles["y_staged", g, h], y_all[:, g, :, half(h)], lo, hi)
 
         def quantize_y(g, h):
-            cols = slice(h * HALF, (h + 1) * HALF)
             nc.vector.quantize_mx(
-                out=y_codes[:, g, cols].bitcast(FP8X4),
-                scales=y_scales[PACK * g : P, cols],
+                out=y_codes[:, g, half(h)].bitcast(FP8X4),
+                scales=y_scales[PACK * g : P, half(h)],
                 in_=tiles["y_staged", g, h][:],
             )
 
-        def store_y(groups, slots):
+        def store_y(g, slots):
             dst = out_0.rearrange("(g p t) m -> p g t m", p=P, t=PACK)
-            nc.sync.dma_start(out=dst[:, groups, slots, :], in_=y_all[:, groups, slots, :])
+            nc.sync.dma_start(out=dst[:, g, slots, :], in_=y_all[:, g, slots, :])
 
-        def store_codes(groups, cols):
+        def store_codes(groups):
             dst = out_1.rearrange("g p m t -> p g (m t)").bitcast(I32)
-            nc.sync.dma_start(out=dst[:, groups, cols], in_=y_codes[:, groups, cols].bitcast(I32))
+            nc.sync.dma_start(out=dst[:, groups, :], in_=y_codes[:, groups, :].bitcast(I32))
+
 
         weight_raw = keep.tile([P, GROUP], BF16, name="weight_raw")
         nc.gpsimd.memset(weight_raw[:], 0.0)
         nc.scalar.dma_start(out=weight_raw[0:GROUPS, :], in_=node_weight.rearrange("(g v) -> g v", g=GROUPS))
         x_raw = keep.tile([P, GROUPS, PACK * F], BF16, name="x_raw")
-        y_all = keep.tile([P, GROUPS, PACK, HID], F32, name="y")
+        y_all = keep.tile([P, GROUPS, PACK, HID], F32, name="y_all")
         y_codes = keep.tile([P, GROUPS, HID], U32, align_bytes=64, name="y_codes")
-        first, second = slice(0, NB_ROWS // 2), slice(NB_ROWS // 2, NB_ROWS)
+        y_scales = keep.tile([P, HID], U8, align_bytes=64, name="y_scales")
+        pair_sums = y_all[:, GROUPS - 1, :, :].rearrange("p t (e f) -> p (t e) f", e=2)
+
+        load_nb_by_node(first)
+        load_nb_by_node(second)
         load_weight("self", w_self)
-        load_x(slice(0, 1))
-        load_nb(0, first)
         load_weight("neigh", w_neigh)
-        load_nb(0, second)
-        load_x(slice(1, 2))
+        load_x(slice(0, 2))
+        load_nb_spread(1, first)
         load_skip(0)
-        load_nb(1, first)
-        load_nb(1, second)
+        load_nb_spread(1, second)
         load_x(slice(2, 4))
         load_skip(1)
-        load_nb(2, first)
-        load_nb(2, second)
+        load_nb_spread(2, first)
+        load_nb_spread(2, second)
 
-        ident = keep.tile([P, P], F32)
+        ident = keep.tile([P, P], F32, name="ident")
         make_identity(nc, ident[:])
-        mean_of = {}
-        for run in (1, 2):
-            members = keep.tile([P, PACK, 8 * run], F32, name="members%d" % run)
-            nc.vector.tensor_reduce(
-                out=members[:],
-                in_=ident[:].rearrange("q (i t n) -> q t i n", t=PACK, n=FAN // run),
-                axis=mybir.AxisListType.X,
-                op=ALU.add,
-            )
-            mean_of[run] = keep.tile([P, PACK, 8 * run], BF16, name="mean_of%d" % run)
-            nc.vector.tensor_scalar(
-                out=mean_of[run][:], in0=members[:], scalar1=1.0 / FAN, scalar2=None, op0=ALU.mult
-            )
+        members = keep.tile([P, PACK, CHUNK // PACK], F32, name="members")
+        nc.vector.tensor_reduce(
+            out=members[:],
+            in_=ident[:].rearrange("q (i t e) -> q t i e", t=PACK, e=FAN // RUN),
+            axis=mybir.AxisListType.X,
+            op=ALU.add,
+        )
+        mean_of = keep.tile([P, PACK, CHUNK // PACK], BF16, name="mean_of")
+        nc.vector.tensor_scalar(out=mean_of[:], in0=members[:], scalar1=1.0 / FAN, scalar2=None, op0=ALU.mult)
         ident_bf = keep.tile([P, P], BF16, name="ident_bf")
         make_identity(nc, ident_bf[:])
-        y_scales = keep.tile([P, HID], U8, align_bytes=64)
 
-        def turn_and_copy_x(g):
-            for a in range(2):
-                turn_x(g, a)
-            for a in range(2):
-                copy_x(g, a)
-
-        def mean_and_copy_nb(g, b):
-            mean_nb(g, b)
-            copy_nb(g, b)
-
-        interleave_weight("self", 0)
-        interleave_weight("self", 1)
-        turn_and_copy_x(0)
+        nb_mean = staged_tile("nb_staged", 2)
+        for a in range(2):
+            add_pairs(a)
+        interleave_weight("self", 0, nc.scalar.copy)
+        for a in range(2):
+            add_pair_sums(a)
+        for a in range(2):
+            divide_sums(a)
+        copy_turned(("nb_staged", 0), "nb_staged", turn(nb_mean))
+        interleave_weight("self", 1, nc.vector.tensor_copy)
+        copy_turned(("x_staged", 0), "x_staged", turn(x_raw[:, 0, :]))
+        interleave_weight("neigh", 1, nc.scalar.copy)
         quantize_weight("self", 0)
-        quantize_weight("self", 1)
-        mean_and_copy_nb(0, 0)
-        mean_and_copy_nb(0, 1)
-        quantize_x(0)
-        interleave_weight("neigh", 0)
-        interleave_weight("neigh", 1)
-        mean_and_copy_nb(0, 2)
-        mean_and_copy_nb(0, 3)
-        quantize_weight("neigh", 0)
+        interleave_weight("neigh", 0, nc.vector.tensor_copy)
         quantize_nb(0)
+        quantize_weight("self", 1)
+        quantize_weight("neigh", 0)
+        quantize_x(0)
         quantize_weight("neigh", 1)
+
         weight_bank = psum.tile([P, PACK, P], BF16, name="weight_bank", tag="turn")
         for t in range(PACK):
             nc.tensor.transpose(weight_bank[:, t, :], weight_raw[:, t:GROUP:PACK], ident_bf[:])
         weight = keep.tile([P, PACK, GROUPS], F32, name="weight")
         nc.scalar.activation(out=weight[:], in_=weight_bank[:, :, 0:GROUPS], func=ACT.Copy)
+
         load_skip(2)
-        load_nb(3, slice(0, NB_ROWS))
+        load_nb_spread(3, both)
         load_skip(3)
 
-        whole = slice(0, HID)
-        for g in range(GROUPS):
-            behind = g > 0
+
+        x_banks = turn(x_raw[:, 1, :])
+        mean_nb(1, 0)
+        copy_turned(("x_staged", 1), "x_staged", x_banks)
+        mean_nb(1, 1)
+        copy_nb(1, 0)
+        copy_nb(1, 1)
+        for step in range(4):
+            products(0, step)
+        relu_skip(0, 0)
+        relu_skip(0, 1)
+        quantize_x(1)
+        mean_nb(1, 2)
+        mean_nb(1, 3)
+        copy_nb(1, 2)
+        copy_nb(1, 3)
+        products(0, 4)
+        products(0, 5)
+        relu_skip(0, 2)
+        relu_skip(0, 3)
+        weigh(0, 0, whole)
+        products(0, 6)
+        products(0, 7)
+        weigh(0, 1, whole)
+        relu_skip(0, 4)
+        relu_skip(0, 5)
+        quantize_nb(1)
+        relu_skip(0, 6)
+        relu_skip(0, 7)
+        weigh(0, 2, whole)
+        weigh(0, 3, whole)
+        store_y(0, slice(0, PACK))
+
+
+        for g in range(1, GROUPS):
             ahead = g + 1 < GROUPS
+            split = SPLIT if ahead else LAST_ROUND_SPLIT
             if ahead:
-                turn_and_copy_x(g + 1)
-            for s in range(4):
-                products(g, s)
+                copy_turned(("x_staged", g + 1), "x_staged", turn(x_raw[:, g + 1, :]))
+            for step in range(4):
+                products(g, step)
             relu_skip(g, 0)
             products(g, 4)
             relu_skip(g, 1)
-            if behind:
-                for h in range(HALVES):
-                    interleave_y(g - 1, h, nc.scalar.copy, SPLIT, HALF)
+            for h in range(HALVES):
+                interleave_y(g - 1, h, nc.scalar.copy, split, HALF)
             relu_skip(g, 2)
             if ahead:
                 quantize_x(g + 1)
                 mean_and_copy_nb(g + 1, 0)
-            if behind:
-                interleave_y(g - 1, 0, nc.vector.tensor_copy, 0, SPLIT)
+            interleave_y(g - 1, 0, nc.vector.tensor_copy, 0, split)
             weigh(g, 0, whole)
             if ahead:
                 mean_and_copy_nb(g + 1, 1)
-            if behind:
-                interleave_y(g - 1, 1, nc.vector.tensor_copy, 0, SPLIT)
+            interleave_y(g - 1, 1, nc.vector.tensor_copy, 0, split)
             if ahead:
                 mean_and_copy_nb(g + 1, 2)
             relu_skip(g, 3)
-            if behind:
-                for h in range(HALVES):
-                    quantize_y(g - 1, h)
-                if g >= 2:
-                    store_codes(slice(0, 2) if ahead else slice(2, 3), whole)
+            for h in range(HALVES):
+                quantize_y(g - 1, h)
+            if g == 2:
+                store_codes(slice(0, 2))
             if ahead:
                 mean_and_copy_nb(g + 1, 3)
-            for s in range(5, 8):
-                products(g, s)
+            else:
+                store_codes(slice(g - 1, g))
+            for step in range(5, 8):
+                products(g, step)
             relu_skip(g, 4)
             weigh(g, 1, whole)
-            if not ahead:
-                store_y(g, slice(0, 2))
-            relu_skip(g, 5)
             if ahead:
+                relu_skip(g, 5)
                 quantize_nb(g + 1)
                 relu_skip(g, 6)
                 weigh(g, 2, whole)
@@ -320,20 +372,26 @@ def tile_graphsage_mean_skip_layer_g2_kernel(
                 weigh(g, 3, whole)
                 store_y(g, slice(0, PACK))
             else:
+                store_y(g, slice(0, 2))
+                relu_skip(g, 5)
                 weigh(g, 2, whole)
                 relu_skip(g, 6)
-                weigh(g, 3, slice(0, HALF))
+                weigh(g, 3, half(0))
                 relu_skip(g, 7)
-                weigh(g, 3, slice(HALF, HID))
-                store_y(g, slice(2, 4))
-        g = GROUPS - 1
-        interleave_y(g, 0, nc.vector.tensor_copy, 0, HALF)
-        interleave_y(g, 1, nc.scalar.copy, LAST_SPLIT, HALF)
-        interleave_y(g, 1, nc.vector.tensor_copy, 0, LAST_SPLIT)
-        quantize_y(g, 0)
-        quantize_y(g, 1)
-        store_codes(g, whole)
-        for q in range(4):
+                weigh(g, 3, half(1))
+                store_y(g, slice(2, PACK))
+
+
+        last = GROUPS - 1
+        interleave_y(last, 0, nc.vector.tensor_copy, 0, TAIL_SPLITS[0])
+        interleave_y(last, 0, nc.scalar.copy, TAIL_SPLITS[0], HALF)
+        interleave_y(last, 1, nc.scalar.copy, TAIL_SPLITS[1], HALF)
+        interleave_y(last, 1, nc.vector.tensor_copy, 0, TAIL_SPLITS[1])
+        for h in range(HALVES):
+            quantize_y(last, h)
+        store_codes(slice(last, GROUPS))
+        for quadrant in range(QUADRANTS):
             nc.scalar.dma_start(
-                out=out_2[:, 4 * q : 4 * q + 4, :].bitcast(I32), in_=y_scales[32 * q : 32 * q + 16, :].bitcast(I32)
+                out=out_2[:, 4 * quadrant : 4 * quadrant + 4, :].bitcast(I32),
+                in_=y_scales[32 * quadrant : 32 * quadrant + 16, :].bitcast(I32),
             )

from contextlib import ExitStack

import concourse.mybir as mybir
from concourse.masks import make_identity

NODES, FAN, F, HID = 2048, 4, 512, 1024
FLOPS = 2 * 2 * NODES * F * HID

F32 = mybir.dt.float32
BF16 = mybir.dt.bfloat16
I32 = mybir.dt.int32
U32 = mybir.dt.uint32
U8 = mybir.dt.uint8
FP8X4 = mybir.dt.float8_e4m3fn_x4
ALU = mybir.AluOpType
ACT = mybir.ActivationFunctionType

P = 128
PACK = 4
GROUP = P * PACK
GROUPS = NODES // GROUP
HALF = 512
HALVES = HID // HALF
NB_ROWS = GROUP * FAN // P
RUN = 2
CHUNK = P * RUN // FAN
BANKS = GROUP // P
QUADRANTS = 4
SPLIT = 384
LAST_ROUND_SPLIT = 320
TAIL_SPLITS = (448, 256)


def tile_graphsage_mean_skip_layer_g2_kernel(
    tc, x, neighbours, w_self, w_neigh, skip, node_weight, out_0, out_1, out_2
):
    nc = tc.nc
    with ExitStack() as ctx:
        keep = ctx.enter_context(tc.tile_pool(name="keep", bufs=1))
        stream = ctx.enter_context(tc.tile_pool(name="stream", bufs=2))
        psum = ctx.enter_context(tc.psum_pool(name="psum", bufs=4))
        ctx.enter_context(tc.manual_schedule())

        nb_rows = neighbours.rearrange("v n f -> (v n) f")
        tiles = {}
        first, second, both = slice(0, NB_ROWS // 2), slice(NB_ROWS // 2, NB_ROWS), slice(0, NB_ROWS)
        whole = slice(0, HID)

        def half(h):
            return slice(h * HALF, (h + 1) * HALF)


        def wide_tile():
            return stream.tile([P, PACK, HID], BF16, name="wide", tag="wide", bufs=4)

        def load_weight(name, w):
            tiles["w_raw", name] = wide_tile()
            nc.sync.dma_start(out=tiles["w_raw", name][:], in_=w.rearrange("(p j) n -> p j n", j=PACK))

        def load_skip(g):
            tiles["skip", g] = wide_tile()
            rows = skip[g * GROUP : (g + 1) * GROUP, :]
            nc.sync.dma_start(out=tiles["skip", g][:], in_=rows.rearrange("(p t) m -> p t m", t=PACK))

        def load_x(groups):
            rows = x.rearrange("(g p t) f -> p g (t f)", p=P, t=PACK)
            nc.sync.dma_start(out=x_raw[:, groups, :], in_=rows[:, groups, :])

        def nb_tile(g):
            if ("nb_raw", g) not in tiles:
                tiles["nb_raw", g] = stream.tile([P, NB_ROWS, F], BF16, name="nb_raw", tag="nb_raw", bufs=3)
            return tiles["nb_raw", g]

        def load_nb_by_node(rows):
            src = nb_rows[0 : NB_ROWS * P, :].rearrange("(p r) f -> p r f", p=P)
            nc.sync.dma_start(out=nb_tile(0)[:, rows, :], in_=src[:, rows, :])

        def load_nb_spread(g, rows):
            src = nb_rows[(g * NB_ROWS + rows.start) * P : (g * NB_ROWS + rows.stop) * P, :]
            nc.sync.dma_start(
                out=nb_tile(g)[:, rows, :].rearrange("q (c s) f -> q c (s f)", s=RUN),
                in_=src.rearrange("(c q s) f -> q c (s f)", q=P, s=RUN),
            )


        def staged_tile(tag, bufs):
            return stream.tile([P, HALF * PACK], BF16, name=tag, tag=tag, bufs=bufs, align_bytes=64)

        def interleave(copy, staged, src, lo, hi):
            copy(
                out=staged[:, PACK * lo : PACK * hi].rearrange("p (c i j) -> p c j i", i=4, j=PACK),
                in_=src[:, :, lo:hi].rearrange("p j (c i) -> p c j i", i=4),
            )

        def quantize(key, staged, tag, bufs):
            codes = stream.tile([P, HALF], U32, name="codes_" + tag, tag="codes_" + tag, bufs=bufs, align_bytes=64)
            scales = stream.tile([P, HALF], U8, name="scales_" + tag, tag="scales_" + tag, bufs=bufs, align_bytes=64)
            nc.vector.quantize_mx(out=codes[:].bitcast(FP8X4), scales=scales[:], in_=staged[:])
            tiles[key] = (codes, scales)

        def interleave_weight(name, h, copy):
            tiles["w_staged", name, h] = staged_tile("staged", 4)
            interleave(copy, tiles["w_staged", name, h], tiles["w_raw", name][:, :, half(h)], 0, HALF)

        def quantize_weight(name, h):
            quantize(("w", name, h), tiles["w_staged", name, h], "w", 2 * HALVES)

        def turn(rows):
            banks = []
            for a in range(2):
                bank = psum.tile([P, 2, 2, P], F32, name="turned", tag="turn")
                for s in range(2):
                    words = rows[:, (2 * a + s) * F : (2 * a + s + 1) * F].bitcast(F32)
                    for u in range(2):
                        nc.tensor.transpose(bank[:, s, u, :], words[:, u : F // 2 : 2], ident[:])
                banks.append(bank)
            return banks

        def copy_turned(key, tag, banks):
            tiles[key] = staged_tile(tag, 2)
            dst = tiles[key][:].bitcast(F32).rearrange("k (t p u) -> k t p u", t=PACK, u=2)
            for a, bank in enumerate(banks):
                nc.scalar.copy(out=dst[:, 2 * a : 2 * a + 2, :, :], in_=bank[:].rearrange("k s u p -> k s p u"))

        def add_pairs(a):
            rows = tiles["nb_raw", 0][:, a * 8 : (a + 1) * 8, :].rearrange("p (r e) f -> p r e f", e=2)
            nc.vector.tensor_tensor(
                out=pair_sums[:, a * 4 : (a + 1) * 4, :], in0=rows[:, :, 0, :], in1=rows[:, :, 1, :], op=ALU.add
            )

        def add_pair_sums(a):
            pairs = pair_sums[:, a * 4 : (a + 1) * 4, :].rearrange("p (t e) f -> p t e f", e=2)
            dst = nb_mean[:, a * 2 * F : (a + 1) * 2 * F].rearrange("p (t f) -> p t f", f=F)
            nc.vector.tensor_tensor(out=dst, in0=pairs[:, :, 0, :], in1=pairs[:, :, 1, :], op=ALU.add)

        def divide_sums(a):
            sums = nb_mean[:, a * 2 * F : (a + 1) * 2 * F]
            nc.vector.tensor_scalar(out=sums, in0=sums, scalar1=1.0 / FAN, scalar2=None, op0=ALU.mult)

        def mean_nb(g, b):
            bank = psum.tile([P, PACK, PACK, P // PACK], F32, name="nb_bank", tag="turn")
            width = CHUNK // PACK
            for c in range(P // CHUNK):
                for j in range(PACK):
                    for s in range(RUN):
                        row = b * FAN + c * RUN + s
                        nc.tensor.matmul(
                            bank[:, j, :, c * width : (c + 1) * width],
                            lhsT=tiles["nb_raw", g][:, row, j:F:PACK],
                            rhs=mean_of[:],
                            start=(s == 0),
                            stop=(s == RUN - 1),
                        )
            tiles["nb_bank", g, b] = bank

        def copy_nb(g, b):
            if b == 0:
                tiles["nb_staged", g] = staged_tile("nb_staged", 2)
            dst = tiles["nb_staged", g][:].rearrange("k (t p j) -> k t p j", t=PACK, j=PACK)
            nc.scalar.copy(
                out=dst[:, :, 32 * b : 32 * b + 32, :],
                in_=tiles["nb_bank", g, b][:].rearrange("k j t i -> k t i j"),
            )

        def mean_and_copy_nb(g, b):
            mean_nb(g, b)
            copy_nb(g, b)

        def quantize_x(g):
            quantize(("nodes", "self", g), tiles["x_staged", g], "x", 2)

        def quantize_nb(g):
            quantize(("nodes", "neigh", g), tiles["nb_staged", g], "nb", 2)


        def products(g, step):
            t, h = divmod(step, HALVES)
            acc = psum.tile([P, HALF], F32, name="acc", tag="acc")
            cols = slice(t * P, (t + 1) * P)
            for i, name in enumerate(("self", "neigh")):
                node_codes, node_scales = tiles["nodes", name, g]
                w_codes, w_scales = tiles["w", name, h]
                nc.tensor.matmul_mx(
                    out=acc[:],
                    lhsT=node_codes[:, cols].bitcast(FP8X4),
                    lhsT_scale=node_scales[:, cols],
                    rhs=w_codes[:].bitcast(FP8X4),
                    rhs_scale=w_scales[:],
                    start=(i == 0),
                    stop=(i == 1),
                )
            tiles["acc", g, step] = acc

        def relu_skip(g, step):
            t, h = divmod(step, HALVES)
            nc.vector.scalar_tensor_tensor(
                out=y_all[:, g, t, half(h)],
                in0=tiles["acc", g, step][:],
                scalar=0.0,
                in1=tiles["skip", g][:, t, half(h)],
                op0=ALU.max,
                op1=ALU.add,
            )

        def weigh(g, t, cols):
            y = y_all[:, g, t, cols]
            nc.scalar.activation(out=y, in_=y, func=ACT.Copy, scale=weight[:, t, g : g + 1])

        def interleave_y(g, h, copy, lo, hi):
            if ("y_staged", g, h) not in tiles:
                tiles["y_staged", g, h] = staged_tile("staged", 4)
            interleave(copy, tiles["y_staged", g, h], y_all[:, g, :, half(h)], lo, hi)

        def quantize_y(g, h):
            nc.vector.quantize_mx(
                out=y_codes[:, g, half(h)].bitcast(FP8X4),
                scales=y_scales[PACK * g : P, half(h)],
                in_=tiles["y_staged", g, h][:],
            )

        def store_y(g, slots):
            dst = out_0.rearrange("(g p t) m -> p g t m", p=P, t=PACK)
            nc.sync.dma_start(out=dst[:, g, slots, :], in_=y_all[:, g, slots, :])

        def store_codes(groups):
            dst = out_1.rearrange("g p m t -> p g (m t)").bitcast(I32)
            nc.sync.dma_start(out=dst[:, groups, :], in_=y_codes[:, groups, :].bitcast(I32))


        weight_raw = keep.tile([P, GROUP], BF16, name="weight_raw")
        nc.gpsimd.memset(weight_raw[:], 0.0)
        nc.scalar.dma_start(out=weight_raw[0:GROUPS, :], in_=node_weight.rearrange("(g v) -> g v", g=GROUPS))
        x_raw = keep.tile([P, GROUPS, PACK * F], BF16, name="x_raw")
        y_all = keep.tile([P, GROUPS, PACK, HID], F32, name="y_all")
        y_codes = keep.tile([P, GROUPS, HID], U32, align_bytes=64, name="y_codes")
        y_scales = keep.tile([P, HID], U8, align_bytes=64, name="y_scales")
        pair_sums = y_all[:, GROUPS - 1, :, :].rearrange("p t (e f) -> p (t e) f", e=2)

        load_nb_by_node(first)
        load_nb_by_node(second)
        load_weight("self", w_self)
        load_weight("neigh", w_neigh)
        load_x(slice(0, 2))
        load_nb_spread(1, first)
        load_skip(0)
        load_nb_spread(1, second)
        load_x(slice(2, 4))
        load_skip(1)
        load_nb_spread(2, first)
        load_nb_spread(2, second)

        ident = keep.tile([P, P], F32, name="ident")
        make_identity(nc, ident[:])
        members = keep.tile([P, PACK, CHUNK // PACK], F32, name="members")
        nc.vector.tensor_reduce(
            out=members[:],
            in_=ident[:].rearrange("q (i t e) -> q t i e", t=PACK, e=FAN // RUN),
            axis=mybir.AxisListType.X,
            op=ALU.add,
        )
        mean_of = keep.tile([P, PACK, CHUNK // PACK], BF16, name="mean_of")
        nc.vector.tensor_scalar(out=mean_of[:], in0=members[:], scalar1=1.0 / FAN, scalar2=None, op0=ALU.mult)
        ident_bf = keep.tile([P, P], BF16, name="ident_bf")
        make_identity(nc, ident_bf[:])

        nb_mean = staged_tile("nb_staged", 2)
        for a in range(2):
            add_pairs(a)
        interleave_weight("self", 0, nc.scalar.copy)
        for a in range(2):
            add_pair_sums(a)
        for a in range(2):
            divide_sums(a)
        copy_turned(("nb_staged", 0), "nb_staged", turn(nb_mean))
        interleave_weight("self", 1, nc.vector.tensor_copy)
        copy_turned(("x_staged", 0), "x_staged", turn(x_raw[:, 0, :]))
        interleave_weight("neigh", 1, nc.scalar.copy)
        quantize_weight("self", 0)
        interleave_weight("neigh", 0, nc.vector.tensor_copy)
        quantize_nb(0)
        quantize_weight("self", 1)
        quantize_weight("neigh", 0)
        quantize_x(0)
        quantize_weight("neigh", 1)

        weight_bank = psum.tile([P, PACK, P], BF16, name="weight_bank", tag="turn")
        for t in range(PACK):
            nc.tensor.transpose(weight_bank[:, t, :], weight_raw[:, t:GROUP:PACK], ident_bf[:])
        weight = keep.tile([P, PACK, GROUPS], F32, name="weight")
        nc.scalar.activation(out=weight[:], in_=weight_bank[:, :, 0:GROUPS], func=ACT.Copy)

        load_skip(2)
        load_nb_spread(3, both)
        load_skip(3)


        x_banks = turn(x_raw[:, 1, :])
        mean_nb(1, 0)
        copy_turned(("x_staged", 1), "x_staged", x_banks)
        mean_nb(1, 1)
        copy_nb(1, 0)
        copy_nb(1, 1)
        for step in range(4):
            products(0, step)
        relu_skip(0, 0)
        relu_skip(0, 1)
        quantize_x(1)
        mean_nb(1, 2)
        mean_nb(1, 3)
        copy_nb(1, 2)
        copy_nb(1, 3)
        products(0, 4)
        products(0, 5)
        relu_skip(0, 2)
        relu_skip(0, 3)
        weigh(0, 0, whole)
        products(0, 6)
        products(0, 7)
        weigh(0, 1, whole)
        relu_skip(0, 4)
        relu_skip(0, 5)
        quantize_nb(1)
        relu_skip(0, 6)
        relu_skip(0, 7)
        weigh(0, 2, whole)
        weigh(0, 3, whole)
        store_y(0, slice(0, PACK))


        for g in range(1, GROUPS):
            ahead = g + 1 < GROUPS
            split = SPLIT if ahead else LAST_ROUND_SPLIT
            if ahead:
                copy_turned(("x_staged", g + 1), "x_staged", turn(x_raw[:, g + 1, :]))
            for step in range(4):
                products(g, step)
            relu_skip(g, 0)
            products(g, 4)
            relu_skip(g, 1)
            for h in range(HALVES):
                interleave_y(g - 1, h, nc.scalar.copy, split, HALF)
            relu_skip(g, 2)
            if ahead:
                quantize_x(g + 1)
                mean_and_copy_nb(g + 1, 0)
            interleave_y(g - 1, 0, nc.vector.tensor_copy, 0, split)
            weigh(g, 0, whole)
            if ahead:
                mean_and_copy_nb(g + 1, 1)
            interleave_y(g - 1, 1, nc.vector.tensor_copy, 0, split)
            if ahead:
                mean_and_copy_nb(g + 1, 2)
            relu_skip(g, 3)
            for h in range(HALVES):
                quantize_y(g - 1, h)
            if g == 2:
                store_codes(slice(0, 2))
            if ahead:
                mean_and_copy_nb(g + 1, 3)
            else:
                store_codes(slice(g - 1, g))
            for step in range(5, 8):
                products(g, step)
            relu_skip(g, 4)
            weigh(g, 1, whole)
            if ahead:
                relu_skip(g, 5)
                quantize_nb(g + 1)
                relu_skip(g, 6)
                weigh(g, 2, whole)
                relu_skip(g, 7)
                weigh(g, 3, whole)
                store_y(g, slice(0, PACK))
            else:
                store_y(g, slice(0, 2))
                relu_skip(g, 5)
                weigh(g, 2, whole)
                relu_skip(g, 6)
                weigh(g, 3, half(0))
                relu_skip(g, 7)
                weigh(g, 3, half(1))
                store_y(g, slice(2, PACK))


        last = GROUPS - 1
        interleave_y(last, 0, nc.vector.tensor_copy, 0, TAIL_SPLITS[0])
        interleave_y(last, 0, nc.scalar.copy, TAIL_SPLITS[0], HALF)
        interleave_y(last, 1, nc.scalar.copy, TAIL_SPLITS[1], HALF)
        interleave_y(last, 1, nc.vector.tensor_copy, 0, TAIL_SPLITS[1])
        for h in range(HALVES):
            quantize_y(last, h)
        store_codes(slice(last, GROUPS))
        for quadrant in range(QUADRANTS):
            nc.scalar.dma_start(
                out=out_2[:, 4 * quadrant : 4 * quadrant + 4, :].bitcast(I32),
                in_=y_scales[32 * quadrant : 32 * quadrant + 16, :].bitcast(I32),
            )
